import numpy as np
import ml_dtypes


def mxq(x, axis, fmt="e4m3"):
    dtype, down = {"e4m3": (ml_dtypes.float8_e4m3fn, 7), "e5m2": (ml_dtypes.float8_e5m2, 14)}[fmt]
    v = np.moveaxis(np.asarray(x, np.float32).astype(ml_dtypes.bfloat16).astype(np.float64), axis, -1)
    blocks = v.reshape(v.shape[:-1] + (-1, 32))
    amax = np.abs(blocks).max(-1, keepdims=True)
    byte = np.maximum(np.where(amax > 0, np.frexp(amax)[1] - 1 + 127, 0) - down, 1)
    scale = np.exp2(byte - 127.0)
    codes = (blocks / scale).astype(np.float32).astype(dtype).astype(np.float64)
    return np.moveaxis((codes * scale).reshape(v.shape), -1, axis)


WIDE = False


def mx_kscale(k):
    if not WIDE:
        return np.ones(k)
    levels = np.array([10, -10, 5, -5, 0])
    if k % 512:
        return np.exp2(np.random.permutation(np.resize(levels, k // 32))).repeat(32)
    a = np.empty((k // 512, 16))
    for p in range(k // 512):
        a[p, :8] = np.random.permutation(np.resize(levels, 8))
        for g in range(8):
            far = levels[np.abs(levels - a[p, g]) >= 10]
            a[p, g + 8] = far[np.random.randint(len(far))]
    return np.exp2(a.ravel()).repeat(32)


def f64(x):
    return np.asarray(x).astype(np.float64)


def striped(idx):
    return np.tile(idx.reshape(-1, 16).T, (8, 1)).astype(np.uint16)


def unstriped(offs):
    return offs[:16].T.reshape(-1).astype(np.int64)


def striped8(idx):
    return np.concatenate([x.reshape(-1, 16).T for x in idx]).astype(np.uint16)


def runs(offs, k):
    lists = np.stack([offs[16 * r : 16 * r + 16].T.reshape(-1) for r in range(8)]).astype(np.int64)
    return lists[np.arange(k) % 512 // 64]


def pack_weight(w):
    k, n = w.shape
    w = f64(np.asarray(w, np.float32).astype(ml_dtypes.bfloat16)).reshape(k // 32, 32, n)
    amax = np.abs(w).max(1)
    byte = np.clip(np.where(amax > 0, np.frexp(amax)[1] - 1 + 127 - 7, 1), 1, 254)
    scaled = (w * np.exp2(127.0 - byte)[:, None, :]).reshape(k, n).astype(np.float32)
    words = np.ascontiguousarray(scaled.reshape(k // 512, 128, 4, n).transpose(0, 1, 3, 2)).astype(ml_dtypes.float8_e4m3fn).view(np.uint8)
    return words, np.ascontiguousarray(byte.astype(np.uint8).reshape(k // 512, 16, n))


def unpack_weight(words, scales):
    g, p, n, _ = words.shape
    vals = np.ascontiguousarray(words).view(ml_dtypes.float8_e4m3fn).astype(np.float64) * np.repeat(np.exp2(scales.astype(np.float64) - 127.0), 8, axis=1)[..., None]
    return vals.transpose(0, 1, 3, 2).reshape(g * 512, n)


E2M1 = np.array([0.0, 0.5, 1.0, 1.5, 2.0, 3.0, 4.0, 6.0, -0.0, -0.5, -1.0, -1.5, -2.0, -3.0, -4.0, -6.0])


def pack_fp4(w):
    k, n = w.shape
    w = f64(np.asarray(w, np.float32).astype(ml_dtypes.bfloat16)).reshape(k // 32, 32, n)
    amax = np.abs(w).max(1)
    mant, ex = np.frexp(amax / 6.0)
    byte = np.clip(np.where(amax > 0, np.where(mant > 0.5, ex, ex - 1) + 127, 1), 1, 254)
    scaled = (w * np.exp2(127.0 - byte)[:, None, :]).reshape(k, n).astype(np.float32)
    c = np.ascontiguousarray(scaled.reshape(k // 512, 128, 4, n).transpose(0, 1, 3, 2)).astype(ml_dtypes.float4_e2m1fn).view(np.uint8) & 0xF
    words = (c[..., 0::2] | (c[..., 1::2] << 4)).reshape(k // 512, 128, 2 * n)
    return np.ascontiguousarray(words), np.ascontiguousarray(byte.astype(np.uint8).reshape(k // 512, 16, n))


def unpack_fp4(words, scales):
    g, _, n = scales.shape
    words = np.ascontiguousarray(words).reshape(g, 128, n, 2)
    nib = np.empty((g, 128, n, 4), np.uint8)
    nib[..., 0::2] = words & 0xF
    nib[..., 1::2] = words >> 4
    vals = E2M1[nib] * np.repeat(np.exp2(scales.astype(np.float64) - 127.0), 8, axis=1)[..., None]
    return vals.transpose(0, 1, 3, 2).reshape(g * 512, n)


def planes(y):
    n, m = y.shape
    v = y.astype(np.float32).astype(ml_dtypes.bfloat16).astype(np.float64).reshape(n // 32, 32, m)
    top = np.abs(v).max(1)
    byte = np.clip(np.where(top > 0, np.frexp(top)[1] - 1 + 127 - 7, 1), 1, 254)
    codes = (v * np.exp2(127.0 - byte)[:, None, :]).reshape(n, m).astype(np.float32).astype(ml_dtypes.float8_e4m3fn).view(np.uint8)
    words = codes.reshape(n // 512, 128, 4, m).transpose(0, 1, 3, 2)
    return np.ascontiguousarray(words), np.ascontiguousarray(byte.astype(np.uint8).reshape(n // 512, 16, m))


K, T, S, H, C = 512, 2048, 512, 512, 512


def setup_inputs():
    n = np.random.standard_normal
    s = mx_kscale(K)[:, None]
    packed_xT = pack_weight(n((K, T)) * s)
    packed_w1 = pack_fp4(n((K, H)) / np.sqrt(K) / s)
    return {
        "x_words": packed_xT[0],
        "x_scales": packed_xT[1],
        "w1_words": packed_w1[0],
        "w1_scales": packed_w1[1],
        "gs": (np.random.uniform(0.5, 1.5, (K, 1)) / s).astype(np.float32),
        "offs": striped(np.random.permutation(T)[:S]),
        "lf": striped8(np.stack([np.random.permutation(S) for _ in range(8)])),
        "rt": striped8(np.stack([np.random.permutation(S) for _ in range(8)])),
        "cand": striped(np.random.permutation(T)[:C]),
    }


def reference(x_words, x_scales, w1_words, w1_scales, gs, offs, lf, rt, cand):
    x_cand = unpack_weight(x_words, x_scales)[:, unstriped(cand)]
    xq = unpack_weight(x_words, x_scales)[:, unstriped(offs)]
    y = unpack_fp4(w1_words, w1_scales).T @ xq
    z = f64(gs) * (0.5 * ((y) ** 2 - ((y[np.arange(H)[:, None], runs(lf, H)]) * (y[np.arange(H)[:, None], runs(rt, H)]))))
    out_0 = 0.0625 * ((x_cand.T @ mxq(z, 0, "e4m3")))
    return (out_0,) + planes(out_0)

@@ -1,0 +1,191 @@
+from contextlib import ExitStack
+
+import concourse.mybir as mybir
+
+K, T, S, H, C = 512, 2048, 512, 512, 512
+FLOPS = 2 * K * H * S + 2 * K * C * S
+
+F32 = mybir.dt.float32
+BF16 = mybir.dt.bfloat16
+I32 = mybir.dt.int32
+U32 = mybir.dt.uint32
+U16 = mybir.dt.uint16
+U8 = mybir.dt.uint8
+FP8X4 = mybir.dt.float8_e4m3fn_x4
+FP4X4 = mybir.dt.float4_e2m1fn_x4
+MULT = mybir.AluOpType.mult
+SUB = mybir.AluOpType.subtract
+COPY = mybir.ActivationFunctionType.Copy
+SQUARE = mybir.ActivationFunctionType.Square
+
+P = 128
+PACK = 4
+BLK = 128
+HALF = 256
+CHUNKS = ((0, 256), (256, 128), (384, 128))
+
+
+def tile_picked_teager8_none_po_kernel(tc, x_words, x_scales, w1_words, w1_scales, gs, offs, lf, rt, cand, out_0, out_1, out_2):
+    nc = tc.nc
+    with ExitStack() as ctx:
+        lists = ctx.enter_context(tc.tile_pool(name="lists", bufs=1))
+        sb = ctx.enter_context(tc.tile_pool(name="sb", bufs=1))
+        ps = ctx.enter_context(tc.psum_pool(name="ps", bufs=1))
+
+        offs_t = lists.tile([P, S // 16], U16, name="offs_t")
+        cand_t = lists.tile([P, C // 16], U16, name="cand_t")
+        lf_t = lists.tile([P, S // 16], U16, name="lf_t")
+        rt_t = lists.tile([P, S // 16], U16, name="rt_t")
+
+        xw = sb.tile([P, T], I32, name="xw", align_bytes=64)
+        xs = sb.tile([P, T], U8, name="xs", align_bytes=64)
+        ww = sb.tile([P, 2 * H], U8, name="ww", align_bytes=64)
+        ws = sb.tile([P, H], U8, name="ws", tag="plane", align_bytes=64)
+        g = sb.tile([P, PACK], F32, name="g", align_bytes=64)
+
+        nc.vector.memset(xs[:].bitcast(I32), 0)
+        nc.vector.memset(ws[:].bitcast(I32), 0)
+
+        nc.sync.dma_start(offs_t[:], offs)
+        nc.sync.dma_start(ww[:].bitcast(I32), w1_words[0].bitcast(I32))
+        nc.sync.dma_start(xw[:], x_words[0].rearrange("p n t -> p (n t)").bitcast(I32))
+        nc.sync.dma_start(cand_t[:], cand)
+        for q in range(4):
+            nc.sync.dma_start(xs[32 * q : 32 * q + 4, :].bitcast(I32), x_scales[0, 4 * q : 4 * q + 4, :].bitcast(I32))
+        for q in range(4):
+            nc.sync.dma_start(ws[32 * q : 32 * q + 4, :].bitcast(I32), w1_scales[0, 4 * q : 4 * q + 4, :].bitcast(I32))
+        nc.sync.dma_start(g[:], gs.rearrange("(p t) o -> p (t o)", t=PACK))
+        nc.sync.dma_start(lf_t[:], lf)
+        nc.sync.dma_start(rt_t[:], rt)
+
+        wwd = sb.tile([P, PACK, P, 2], U8, name="wwd", align_bytes=64)
+        wsd = sb.tile([P, PACK, P], U8, name="wsd", align_bytes=64)
+        xqw = sb.tile([P, S], U32, name="xqw", align_bytes=64)
+        xqs = sb.tile([P, S], U8, name="xqs", align_bytes=64)
+        xcw = sb.tile([P, C], U32, name="xcw", align_bytes=64)
+        xcs = sb.tile([P, C], U8, name="xcs", tag="plane", align_bytes=64)
+        xcwd = sb.tile([P, PACK, P], U32, name="xcwd", align_bytes=64)
+        xcsd = sb.tile([P, PACK, P], U8, name="xcsd", align_bytes=64)
+
+        nc.vector.tensor_copy(wwd[:], ww[:].rearrange("p (m t b) -> p t m b", t=PACK, b=2))
+        nc.vector.tensor_copy(xqw[:], xw[:].bitcast(U32).indirect(offs_t[:]))
+        nc.vector.tensor_copy(xcw[:], xw[:].bitcast(U32).indirect(cand_t[:]))
+        nc.vector.tensor_copy(xqs[:], xs[:].indirect(offs_t[:]))
+        nc.vector.tensor_copy(wsd[:], ws[:].rearrange("p (m t) -> p t m", t=PACK))
+        nc.vector.tensor_copy(xcs[:], xs[:].indirect(cand_t[:]))
+        nc.vector.tensor_copy(xcwd[:].bitcast(I32), xcw[:].bitcast(I32).rearrange("p (m t) -> p t m", t=PACK))
+        nc.vector.tensor_copy(xcsd[:], xcs[:].rearrange("p (m t) -> p t m", t=PACK))
+
+        hg = sb.tile([P, PACK, HALF], F32, name="hg", align_bytes=64)
+        nc.scalar.activation(hg[:], g[:].unsqueeze(2).to_broadcast([P, PACK, HALF]), COPY, scale=0.5)
+
+        yp = [ps.tile([P, S], F32, name="yp%d" % t) for t in range(PACK)]
+        y = [sb.tile([P, S], F32, name="y%d" % t, align_bytes=64) for t in range(PACK)]
+        for t in range(PACK):
+            nc.tensor.matmul_mx(
+                out=yp[t][:],
+                lhsT=wwd[:, t].rearrange("p m b -> p (m b)").bitcast(FP4X4),
+                lhsT_scale=wsd[:, t, :],
+                rhs=xqw[:].bitcast(FP8X4),
+                rhs_scale=xqs[:],
+                start=True,
+                stop=True,
+            )
+            nc.scalar.activation(y[t][:], yp[t][:], COPY)
+
+        sq = [sb.tile([P, PACK, HALF], F32, name="sq%d" % u, align_bytes=64) for u in range(2)]
+        hsq = [sb.tile([P, PACK, HALF], F32, name="hsq%d" % u, align_bytes=64) for u in range(2)]
+        for u in range(2):
+            for t in range(PACK):
+                nc.scalar.activation(sq[u][:, t, :], yp[t][:, u * HALF : (u + 1) * HALF], SQUARE)
+            for t in range(PACK):
+                nc.scalar.activation(hsq[u][:, t, :], sq[u][:, t, :], COPY, scale=hg[:, t, 0:1])
+
+        ow = sb.tile([P, S], U32, name="ow", align_bytes=64)
+        osc = sb.tile([P, S], U8, name="osc", align_bytes=64)
+        out0 = out_0.rearrange("(p t) j -> p t j", t=PACK)
+        out1 = out_1[0].rearrange("p n t -> p (n t)").bitcast(I32)
+
+        prod = {}
+        left = {}
+        zq = {}
+        ob = {}
+
+        def gather_left(c, t):
+            c0, n = CHUNKS[c]
+            left[c, t] = sb.tile([P, n], F32, name="left%d_%d" % (c, t), tag="left", bufs=3, align_bytes=64)
+            nc.vector.tensor_tensor(left[c, t][:], y[t][:].indirect(lf_t[:, c0 // 16 : (c0 + n) // 16]), hg[:, t, 0:n], MULT)
+
+        def gather_right(c, t):
+            c0, n = CHUNKS[c]
+            if t == 0:
+                prod[c] = sb.tile([P, PACK, n], F32, name="prod%d" % c, tag="prod", align_bytes=64)
+            nc.vector.tensor_tensor(prod[c][:, t, :], y[t][:].indirect(rt_t[:, c0 // 16 : (c0 + n) // 16]), left[c, t][:], MULT)
+
+        def energy(c):
+            c0, n = CHUNKS[c]
+            zb = sb.tile([P, n, PACK], BF16, name="zb%d" % c, align_bytes=64)
+            h0 = c0 % HALF
+            nc.vector.tensor_tensor(
+                zb[:].rearrange("p (c i) t -> p c t i", i=4),
+                hsq[c0 // HALF][:, :, h0 : h0 + n].rearrange("p t (c i) -> p c t i", i=4),
+                prod[c][:].rearrange("p t (c i) -> p c t i", i=4),
+                SUB,
+            )
+            return zb
+
+        def quantize_energy(c, zb):
+            n = CHUNKS[c][1]
+            zw = sb.tile([P, n], U32, name="zw%d" % c, align_bytes=64)
+            zs = sb.tile([P, n], U8, name="zs%d" % c, align_bytes=64)
+            nc.vector.quantize_mx(out=zw[:].bitcast(FP8X4), scales=zs[:], in_=zb[:].rearrange("p n t -> p (n t)"))
+            zq[c] = (zw, zs)
+
+        def score(c):
+            c0, n = CHUNKS[c]
+            zw, zs = zq[c]
+            ob[c] = sb.tile([P, n, PACK], BF16, name="ob%d" % c, align_bytes=64)
+            for b0 in range(0, n, BLK):
+                op = ps.tile([P, PACK, BLK], F32, name="op%d" % (c0 + b0))
+                for t in range(PACK):
+                    nc.tensor.matmul_mx(
+                        out=op[:, t, :],
+                        lhsT=xcwd[:, t, :].bitcast(FP8X4),
+                        lhsT_scale=xcsd[:, t, :],
+                        rhs=zw[:, b0 : b0 + BLK].bitcast(FP8X4),
+                        rhs_scale=zs[:, b0 : b0 + BLK],
+                        start=True,
+                        stop=True,
+                    )
+                nc.scalar.activation(ob[c][:, b0 : b0 + BLK, :], op[:].rearrange("p t n -> p n t"), COPY, scale=0.0625)
+                of = sb.tile([P, PACK, BLK], F32, name="of%d" % (c0 + b0), align_bytes=64)
+                nc.scalar.activation(of[:], op[:], COPY, scale=0.0625)
+                nc.sync.dma_start(out0[:, :, c0 + b0 : c0 + b0 + BLK], of[:])
+
+        def quantize_out(c):
+            c0, n = CHUNKS[c]
+            nc.vector.quantize_mx(
+                out=ow[:, c0 : c0 + n].bitcast(FP8X4),
+                scales=osc[:, c0 : c0 + n],
+                in_=ob[c][:].rearrange("p n t -> p (n t)"),
+            )
+            nc.sync.dma_start(out1[:, c0 : c0 + n], ow[:, c0 : c0 + n].bitcast(I32))
+
+        steps = [(c, t) for c in range(len(CHUNKS)) for t in range(PACK)]
+        zb = {}
+        for i in range(len(steps) + 3):
+            if i < len(steps):
+                gather_left(*steps[i])
+            if 1 <= i <= len(steps):
+                gather_right(*steps[i - 1])
+            if i >= 5 and (i - 5) % PACK == 0:
+                zb[(i - 5) // PACK] = energy((i - 5) // PACK)
+            if i >= 6 and (i - 6) % PACK == 0:
+                c = (i - 6) // PACK
+                quantize_energy(c, zb[c])
+                score(c)
+                if c >= 1:
+                    quantize_out(c - 1)
+        quantize_out(len(CHUNKS) - 1)
+        for q in range(4):
+            nc.sync.dma_start(out_2[0, 4 * q : 4 * q + 4, :].bitcast(I32), osc[32 * q : 32 * q + 4, :].bitcast(I32))

@@ -21,8 +21,9 @@ SQUARE = mybir.ActivationFunctionType.Square
 P = 128
 PACK = 4
 BLK = 128
-HALF = 256
-CHUNKS = ((0, 256), (256, 128), (384, 128))
+HEAD = S - BLK
+WHOLE = 2
+OUT_SCALE = 0.0625
 
 
 def tile_picked_teager8_none_po_kernel(tc, x_words, x_scales, w1_words, w1_scales, gs, offs, lf, rt, cand, out_0, out_1, out_2):
@@ -40,21 +41,21 @@ def tile_picked_teager8_none_po_kernel(tc, x_words, x_scales, w1_words, w1_scale
         xw = sb.tile([P, T], I32, name="xw", align_bytes=64)
         xs = sb.tile([P, T], U8, name="xs", align_bytes=64)
         ww = sb.tile([P, 2 * H], U8, name="ww", align_bytes=64)
-        ws = sb.tile([P, H], U8, name="ws", tag="plane", align_bytes=64)
+        ws = sb.tile([P, H], U8, name="ws", tag="staging", align_bytes=64)
         g = sb.tile([P, PACK], F32, name="g", align_bytes=64)
 
         nc.vector.memset(xs[:].bitcast(I32), 0)
-        nc.vector.memset(ws[:].bitcast(I32), 0)
+        nc.gpsimd.memset(ws[:].bitcast(I32), 0)
 
         nc.sync.dma_start(offs_t[:], offs)
-        nc.sync.dma_start(ww[:].bitcast(I32), w1_words[0].bitcast(I32))
-        nc.sync.dma_start(xw[:], x_words[0].rearrange("p n t -> p (n t)").bitcast(I32))
         nc.sync.dma_start(cand_t[:], cand)
+        nc.sync.dma_start(ww[:].bitcast(I32), w1_words[0].bitcast(I32))
         for q in range(4):
             nc.sync.dma_start(xs[32 * q : 32 * q + 4, :].bitcast(I32), x_scales[0, 4 * q : 4 * q + 4, :].bitcast(I32))
+        nc.sync.dma_start(xw[:], x_words[0].rearrange("p n t -> p (n t)").bitcast(I32))
+        nc.sync.dma_start(g[:], gs.rearrange("(p t) o -> p (t o)", t=PACK))
         for q in range(4):
             nc.sync.dma_start(ws[32 * q : 32 * q + 4, :].bitcast(I32), w1_scales[0, 4 * q : 4 * q + 4, :].bitcast(I32))
-        nc.sync.dma_start(g[:], gs.rearrange("(p t) o -> p (t o)", t=PACK))
         nc.sync.dma_start(lf_t[:], lf)
         nc.sync.dma_start(rt_t[:], rt)
 
@@ -62,25 +63,28 @@ def tile_picked_teager8_none_po_kernel(tc, x_words, x_scales, w1_words, w1_scale
         wsd = sb.tile([P, PACK, P], U8, name="wsd", align_bytes=64)
         xqw = sb.tile([P, S], U32, name="xqw", align_bytes=64)
         xqs = sb.tile([P, S], U8, name="xqs", align_bytes=64)
-        xcw = sb.tile([P, C], U32, name="xcw", align_bytes=64)
-        xcs = sb.tile([P, C], U8, name="xcs", tag="plane", align_bytes=64)
+        xcw = sb.tile([P, C], U32, name="xcw", tag="staging", align_bytes=64)
+        xcs = sb.tile([P, C], U8, name="xcs", align_bytes=64)
         xcwd = sb.tile([P, PACK, P], U32, name="xcwd", align_bytes=64)
         xcsd = sb.tile([P, PACK, P], U8, name="xcsd", align_bytes=64)
 
-        nc.vector.tensor_copy(wwd[:], ww[:].rearrange("p (m t b) -> p t m b", t=PACK, b=2))
-        nc.vector.tensor_copy(xqw[:], xw[:].bitcast(U32).indirect(offs_t[:]))
-        nc.vector.tensor_copy(xcw[:], xw[:].bitcast(U32).indirect(cand_t[:]))
         nc.vector.tensor_copy(xqs[:], xs[:].indirect(offs_t[:]))
-        nc.vector.tensor_copy(wsd[:], ws[:].rearrange("p (m t) -> p t m", t=PACK))
         nc.vector.tensor_copy(xcs[:], xs[:].indirect(cand_t[:]))
-        nc.vector.tensor_copy(xcwd[:].bitcast(I32), xcw[:].bitcast(I32).rearrange("p (m t) -> p t m", t=PACK))
+        nc.vector.tensor_copy(wwd[:], ww[:].rearrange("p (m t b) -> p t m b", t=PACK, b=2))
         nc.vector.tensor_copy(xcsd[:], xcs[:].rearrange("p (m t) -> p t m", t=PACK))
+        nc.vector.tensor_copy(xqw[:], xw[:].bitcast(U32).indirect(offs_t[:]))
+        nc.vector.tensor_copy(wsd[:], ws[:].rearrange("p (m t) -> p t m", t=PACK))
+        nc.vector.tensor_copy(xcw[:], xw[:].bitcast(U32).indirect(cand_t[:]))
+        nc.vector.tensor_copy(xcwd[:].bitcast(I32), xcw[:].bitcast(I32).rearrange("p (m t) -> p t m", t=PACK))
 
-        hg = sb.tile([P, PACK, HALF], F32, name="hg", align_bytes=64)
-        nc.scalar.activation(hg[:], g[:].unsqueeze(2).to_broadcast([P, PACK, HALF]), COPY, scale=0.5)
+        win = [sb.tile([P, 2 * S if t < WHOLE else S], F32, name="win%d" % t, align_bytes=64) for t in range(PACK)]
+        hg_rest = sb.tile([P, PACK - WHOLE, HEAD], F32, name="hg_rest", align_bytes=64)
+        hg = [win[(t + 1) % WHOLE][:, S : 2 * S] for t in range(WHOLE)] + [hg_rest[:, t, :] for t in range(PACK - WHOLE)]
+        for t in range(WHOLE):
+            nc.scalar.activation(hg[t], g[:, t : t + 1].to_broadcast([P, S]), COPY, scale=0.5)
+        nc.scalar.activation(hg_rest[:], g[:, WHOLE:PACK].unsqueeze(2).to_broadcast([P, PACK - WHOLE, HEAD]), COPY, scale=0.5)
 
         yp = [ps.tile([P, S], F32, name="yp%d" % t) for t in range(PACK)]
-        y = [sb.tile([P, S], F32, name="y%d" % t, align_bytes=64) for t in range(PACK)]
         for t in range(PACK):
             nc.tensor.matmul_mx(
                 out=yp[t][:],
@@ -91,101 +95,133 @@ def tile_picked_teager8_none_po_kernel(tc, x_words, x_scales, w1_words, w1_scale
                 start=True,
                 stop=True,
             )
-            nc.scalar.activation(y[t][:], yp[t][:], COPY)
+            nc.scalar.activation(win[t][:, 0:S], yp[t][:], COPY)
 
-        sq = [sb.tile([P, PACK, HALF], F32, name="sq%d" % u, align_bytes=64) for u in range(2)]
-        hsq = [sb.tile([P, PACK, HALF], F32, name="hsq%d" % u, align_bytes=64) for u in range(2)]
-        for u in range(2):
+        hsq = {}
+        for c0, n in ((0, BLK), (BLK, HEAD)):
+            sq = sb.tile([P, PACK, n], F32, name="sq%d" % c0, align_bytes=64)
+            hsq[c0] = sb.tile([P, PACK, n], F32, name="hsq%d" % c0, align_bytes=64)
             for t in range(PACK):
-                nc.scalar.activation(sq[u][:, t, :], yp[t][:, u * HALF : (u + 1) * HALF], SQUARE)
+                nc.scalar.activation(sq[:, t, :], yp[t][:, c0 : c0 + n], SQUARE)
             for t in range(PACK):
-                nc.scalar.activation(hsq[u][:, t, :], sq[u][:, t, :], COPY, scale=hg[:, t, 0:1])
+                nc.scalar.activation(hsq[c0][:, t, :], sq[:, t, :], COPY, scale=hg[t][:, 0:1])
 
         ow = sb.tile([P, S], U32, name="ow", align_bytes=64)
         osc = sb.tile([P, S], U8, name="osc", align_bytes=64)
         out0 = out_0.rearrange("(p t) j -> p t j", t=PACK)
         out1 = out_1[0].rearrange("p n t -> p (n t)").bitcast(I32)
 
-        prod = {}
+        prod = sb.tile([P, PACK, S], F32, name="prod", align_bytes=64)
         left = {}
-        zq = {}
+        zb = {}
         ob = {}
 
-        def gather_left(c, t):
-            c0, n = CHUNKS[c]
-            left[c, t] = sb.tile([P, n], F32, name="left%d_%d" % (c, t), tag="left", bufs=3, align_bytes=64)
-            nc.vector.tensor_tensor(left[c, t][:], y[t][:].indirect(lf_t[:, c0 // 16 : (c0 + n) // 16]), hg[:, t, 0:n], MULT)
+        def gather_left(t, c0, n):
+            left[t, c0] = sb.tile([P, n], F32, name="left%d_%d" % (t, c0), tag="left", bufs=3, align_bytes=64)
+            nc.vector.tensor_tensor(left[t, c0][:], win[t][:].indirect(lf_t[:, c0 // 16 : (c0 + n) // 16]), hg[t][:, 0:n], MULT)
 
-        def gather_right(c, t):
-            c0, n = CHUNKS[c]
-            if t == 0:
-                prod[c] = sb.tile([P, PACK, n], F32, name="prod%d" % c, tag="prod", align_bytes=64)
-            nc.vector.tensor_tensor(prod[c][:, t, :], y[t][:].indirect(rt_t[:, c0 // 16 : (c0 + n) // 16]), left[c, t][:], MULT)
+        def gather_right(t, c0, n):
+            nc.vector.tensor_tensor(prod[:, t, c0 : c0 + n], win[t][:].indirect(rt_t[:, c0 // 16 : (c0 + n) // 16]), left[t, c0][:], MULT)
 
-        def energy(c):
-            c0, n = CHUNKS[c]
-            zb = sb.tile([P, n, PACK], BF16, name="zb%d" % c, align_bytes=64)
-            h0 = c0 % HALF
+        def energy(c0, n):
+            h0 = min(c0, BLK)
+            zb[c0] = sb.tile([P, n, PACK], BF16, name="zb%d" % c0, align_bytes=64)
             nc.vector.tensor_tensor(
-                zb[:].rearrange("p (c i) t -> p c t i", i=4),
-                hsq[c0 // HALF][:, :, h0 : h0 + n].rearrange("p t (c i) -> p c t i", i=4),
-                prod[c][:].rearrange("p t (c i) -> p c t i", i=4),
+                zb[c0][:].rearrange("p (c i) t -> p c t i", i=4),
+                hsq[h0][:, :, c0 - h0 : c0 - h0 + n].rearrange("p t (c i) -> p c t i", i=4),
+                prod[:, :, c0 : c0 + n].rearrange("p t (c i) -> p c t i", i=4),
                 SUB,
             )
-            return zb
 
-        def quantize_energy(c, zb):
-            n = CHUNKS[c][1]
-            zw = sb.tile([P, n], U32, name="zw%d" % c, align_bytes=64)
-            zs = sb.tile([P, n], U8, name="zs%d" % c, align_bytes=64)
-            nc.vector.quantize_mx(out=zw[:].bitcast(FP8X4), scales=zs[:], in_=zb[:].rearrange("p n t -> p (n t)"))
-            zq[c] = (zw, zs)
+        def quantize_energy(c0, n):
+            zw = sb.tile([P, n], U32, name="zw%d" % c0, align_bytes=64)
+            zs = sb.tile([P, n], U8, name="zs%d" % c0, align_bytes=64)
+            nc.vector.quantize_mx(out=zw[:].bitcast(FP8X4), scales=zs[:], in_=zb[c0][:].rearrange("p n t -> p (n t)"))
+            return zw, zs
 
-        def score(c):
-            c0, n = CHUNKS[c]
-            zw, zs = zq[c]
-            ob[c] = sb.tile([P, n, PACK], BF16, name="ob%d" % c, align_bytes=64)
-            for b0 in range(0, n, BLK):
-                op = ps.tile([P, PACK, BLK], F32, name="op%d" % (c0 + b0))
-                for t in range(PACK):
-                    nc.tensor.matmul_mx(
-                        out=op[:, t, :],
-                        lhsT=xcwd[:, t, :].bitcast(FP8X4),
-                        lhsT_scale=xcsd[:, t, :],
-                        rhs=zw[:, b0 : b0 + BLK].bitcast(FP8X4),
-                        rhs_scale=zs[:, b0 : b0 + BLK],
-                        start=True,
-                        stop=True,
-                    )
-                nc.scalar.activation(ob[c][:, b0 : b0 + BLK, :], op[:].rearrange("p t n -> p n t"), COPY, scale=0.0625)
-                of = sb.tile([P, PACK, BLK], F32, name="of%d" % (c0 + b0), align_bytes=64)
-                nc.scalar.activation(of[:], op[:], COPY, scale=0.0625)
-                nc.sync.dma_start(out0[:, :, c0 + b0 : c0 + b0 + BLK], of[:])
-
-        def quantize_out(c):
-            c0, n = CHUNKS[c]
-            nc.vector.quantize_mx(
-                out=ow[:, c0 : c0 + n].bitcast(FP8X4),
-                scales=osc[:, c0 : c0 + n],
-                in_=ob[c][:].rearrange("p n t -> p (n t)"),
+        def score(out, t, zw, zs):
+            nc.tensor.matmul_mx(
+                out=out,
+                lhsT=xcwd[:, t, :].bitcast(FP8X4),
+                lhsT_scale=xcsd[:, t, :],
+                rhs=zw.bitcast(FP8X4),
+                rhs_scale=zs,
+                start=True,
+                stop=True,
             )
-            nc.sync.dma_start(out1[:, c0 : c0 + n], ow[:, c0 : c0 + n].bitcast(I32))
 
-        steps = [(c, t) for c in range(len(CHUNKS)) for t in range(PACK)]
-        zb = {}
-        for i in range(len(steps) + 3):
-            if i < len(steps):
-                gather_left(*steps[i])
-            if 1 <= i <= len(steps):
-                gather_right(*steps[i - 1])
-            if i >= 5 and (i - 5) % PACK == 0:
-                zb[(i - 5) // PACK] = energy((i - 5) // PACK)
-            if i >= 6 and (i - 6) % PACK == 0:
-                c = (i - 6) // PACK
-                quantize_energy(c, zb[c])
-                score(c)
-                if c >= 1:
-                    quantize_out(c - 1)
-        quantize_out(len(CHUNKS) - 1)
+        def score_block(c0):
+            zw, zs = quantize_energy(c0, BLK)
+            bank = ps.tile([P, PACK, BLK], F32, name="op%d" % c0, tag="op", bufs=4)
+            for t in range(PACK):
+                score(bank[:, t, :], t, zw[:], zs[:])
+            return bank
+
+        def round_block(dst, bank, on_vector=False):
+            woven = bank[:].rearrange("p t n -> p n t")
+            if on_vector:
+                nc.vector.tensor_scalar(dst, woven, OUT_SCALE, None, MULT)
+            else:
+                nc.scalar.activation(dst, woven, COPY, scale=OUT_SCALE)
+
+        def store_block(c0, bank):
+            of = sb.tile([P, PACK, BLK], F32, name="of%d" % c0, align_bytes=64)
+            nc.scalar.activation(of[:], bank[:], COPY, scale=OUT_SCALE)
+            nc.sync.dma_start(out0[:, :, c0 : c0 + BLK], of[:])
+
+        def score_last():
+            zw, zs = quantize_energy(HEAD, BLK)
+            of = sb.tile([P, PACK, BLK], F32, name="of_last", align_bytes=64)
+            for t0 in (0, 2):
+                bank = ps.tile([P, 2, BLK], F32, name="op_last%d" % t0, tag="op", bufs=4)
+                for t in (t0, t0 + 1):
+                    score(bank[:, t - t0, :], t, zw[:], zs[:])
+                nc.scalar.activation(of[:, t0 : t0 + 2, :], bank[:], COPY, scale=OUT_SCALE)
+            nc.sync.dma_start(out0[:, :, HEAD:S], of[:])
+            return of
+
+        def quantize_out(c0, n):
+            cols = slice(c0, c0 + n)
+            nc.vector.quantize_mx(out=ow[:, cols].bitcast(FP8X4), scales=osc[:, cols], in_=ob[c0][:].rearrange("p n t -> p (n t)"))
+            nc.sync.dma_start(out1[:, cols], ow[:, cols].bitcast(I32))
+
+        whole = [(t, 0, S) for t in range(WHOLE)]
+        head = [(t, 0, HEAD) for t in range(WHOLE, PACK)]
+        last = [(t, HEAD, BLK) for t in range(WHOLE, PACK)]
+        early = whole + head
+        gather_left(*early[0])
+        for i in range(1, PACK):
+            gather_left(*early[i])
+            gather_right(*early[i - 1])
+        gather_left(*last[0])
+        gather_right(*early[-1])
+        gather_left(*last[1])
+        ob[0] = sb.tile([P, BLK, PACK], BF16, name="ob0", align_bytes=64)
+        ob[BLK] = sb.tile([P, 2 * BLK, PACK], BF16, name="ob1", align_bytes=64)
+        energy(0, BLK)
+        gather_right(*last[0])
+        bank0 = score_block(0)
+        round_block(ob[0][:], bank0)
+        store_block(0, bank0)
+        energy(BLK, BLK)
+        gather_right(*last[1])
+        bank1 = score_block(BLK)
+        round_block(ob[BLK][:, 0:BLK, :], bank1)
+        store_block(BLK, bank1)
+        energy(2 * BLK, BLK)
+        energy(HEAD, BLK)
+        bank2 = score_block(2 * BLK)
+        of_last = score_last()
+        quantize_out(0, BLK)
+        round_block(ob[BLK][:, BLK : 2 * BLK, :], bank2, on_vector=True)
+        store_block(2 * BLK, bank2)
+        quantize_out(BLK, 2 * BLK)
+        ob[HEAD] = sb.tile([P, BLK, PACK], BF16, name="ob_last", align_bytes=64)
+        nc.vector.tensor_copy(
+            ob[HEAD][:].rearrange("p (c i) t -> p c t i", i=4),
+            of_last[:].rearrange("p t (c i) -> p c t i", i=4),
+        )
+        quantize_out(HEAD, BLK)
         for q in range(4):
-            nc.sync.dma_start(out_2[0, 4 * q : 4 * q + 4, :].bitcast(I32), osc[32 * q : 32 * q + 4, :].bitcast(I32))
+            queue = nc.sync if q < 2 else nc.scalar
+            queue.dma_start(out_2[0, 4 * q : 4 * q + 4, :].bitcast(I32), osc[32 * q : 32 * q + 4, :].bitcast(I32))

@@ -47,15 +47,16 @@ def tile_picked_teager8_none_po_kernel(tc, x_words, x_scales, w1_words, w1_scale
         nc.vector.memset(xs[:].bitcast(I32), 0)
         nc.gpsimd.memset(ws[:].bitcast(I32), 0)
 
-        nc.sync.dma_start(offs_t[:], offs)
-        nc.sync.dma_start(cand_t[:], cand)
         nc.sync.dma_start(ww[:].bitcast(I32), w1_words[0].bitcast(I32))
+        nc.sync.dma_start(offs_t[:], offs)
         for q in range(4):
-            nc.sync.dma_start(xs[32 * q : 32 * q + 4, :].bitcast(I32), x_scales[0, 4 * q : 4 * q + 4, :].bitcast(I32))
+            queue = nc.sync if q % 2 == 0 else nc.scalar
+            queue.dma_start(xs[32 * q : 32 * q + 4, :].bitcast(I32), x_scales[0, 4 * q : 4 * q + 4, :].bitcast(I32))
+        nc.sync.dma_start(cand_t[:], cand)
         nc.sync.dma_start(xw[:], x_words[0].rearrange("p n t -> p (n t)").bitcast(I32))
-        nc.sync.dma_start(g[:], gs.rearrange("(p t) o -> p (t o)", t=PACK))
         for q in range(4):
             nc.sync.dma_start(ws[32 * q : 32 * q + 4, :].bitcast(I32), w1_scales[0, 4 * q : 4 * q + 4, :].bitcast(I32))
+        nc.sync.dma_start(g[:], gs.rearrange("(p t) o -> p (t o)", t=PACK))
         nc.sync.dma_start(lf_t[:], lf)
         nc.sync.dma_start(rt_t[:], rt)
 
@@ -127,9 +128,9 @@ def tile_picked_teager8_none_po_kernel(tc, x_words, x_scales, w1_words, w1_scale
             h0 = min(c0, BLK)
             zb[c0] = sb.tile([P, n, PACK], BF16, name="zb%d" % c0, align_bytes=64)
             nc.vector.tensor_tensor(
-                zb[c0][:].rearrange("p (c i) t -> p c t i", i=4),
-                hsq[h0][:, :, c0 - h0 : c0 - h0 + n].rearrange("p t (c i) -> p c t i", i=4),
-                prod[:, :, c0 : c0 + n].rearrange("p t (c i) -> p c t i", i=4),
+                zb[c0][:].rearrange("p (c i) t -> p c t i", i=2),
+                hsq[h0][:, :, c0 - h0 : c0 - h0 + n].rearrange("p t (c i) -> p c t i", i=2),
+                prod[:, :, c0 : c0 + n].rearrange("p t (c i) -> p c t i", i=2),
                 SUB,
             )
 
@@ -218,8 +219,8 @@ def tile_picked_teager8_none_po_kernel(tc, x_words, x_scales, w1_words, w1_scale
         quantize_out(BLK, 2 * BLK)
         ob[HEAD] = sb.tile([P, BLK, PACK], BF16, name="ob_last", align_bytes=64)
         nc.vector.tensor_copy(
-            ob[HEAD][:].rearrange("p (c i) t -> p c t i", i=4),
-            of_last[:].rearrange("p t (c i) -> p c t i", i=4),
+            ob[HEAD][:].rearrange("p (c i) t -> p c t i", i=2),
+            of_last[:].rearrange("p t (c i) -> p c t i", i=2),
         )
         quantize_out(HEAD, BLK)
         for q in range(4):

@@ -41,18 +41,17 @@ def tile_picked_teager8_none_po_kernel(tc, x_words, x_scales, w1_words, w1_scale
         xw = sb.tile([P, T], I32, name="xw", align_bytes=64)
         xs = sb.tile([P, T], U8, name="xs", align_bytes=64)
         ww = sb.tile([P, 2 * H], U8, name="ww", align_bytes=64)
-        ws = sb.tile([P, H], U8, name="ws", tag="staging", align_bytes=64)
+        ws = sb.tile([P, H], U8, name="ws", align_bytes=64)
         g = sb.tile([P, PACK], F32, name="g", align_bytes=64)
 
         nc.vector.memset(xs[:].bitcast(I32), 0)
         nc.gpsimd.memset(ws[:].bitcast(I32), 0)
 
         nc.sync.dma_start(ww[:].bitcast(I32), w1_words[0].bitcast(I32))
-        nc.sync.dma_start(offs_t[:], offs)
-        for q in range(4):
-            queue = nc.sync if q % 2 == 0 else nc.scalar
-            queue.dma_start(xs[32 * q : 32 * q + 4, :].bitcast(I32), x_scales[0, 4 * q : 4 * q + 4, :].bitcast(I32))
         nc.sync.dma_start(cand_t[:], cand)
+        for q in range(4):
+            nc.sync.dma_start(xs[32 * q : 32 * q + 4, :].bitcast(I32), x_scales[0, 4 * q : 4 * q + 4, :].bitcast(I32))
+        nc.sync.dma_start(offs_t[:], offs)
         nc.sync.dma_start(xw[:], x_words[0].rearrange("p n t -> p (n t)").bitcast(I32))
         for q in range(4):
             nc.sync.dma_start(ws[32 * q : 32 * q + 4, :].bitcast(I32), w1_scales[0, 4 * q : 4 * q + 4, :].bitcast(I32))
@@ -64,17 +63,18 @@ def tile_picked_teager8_none_po_kernel(tc, x_words, x_scales, w1_words, w1_scale
         wsd = sb.tile([P, PACK, P], U8, name="wsd", align_bytes=64)
         xqw = sb.tile([P, S], U32, name="xqw", align_bytes=64)
         xqs = sb.tile([P, S], U8, name="xqs", align_bytes=64)
-        xcw = sb.tile([P, C], U32, name="xcw", tag="staging", align_bytes=64)
+        xcw = sb.tile([P, C], U32, name="xcw", align_bytes=64)
         xcs = sb.tile([P, C], U8, name="xcs", align_bytes=64)
         xcwd = sb.tile([P, PACK, P], U32, name="xcwd", align_bytes=64)
         xcsd = sb.tile([P, PACK, P], U8, name="xcsd", align_bytes=64)
 
-        nc.vector.tensor_copy(xqs[:], xs[:].indirect(offs_t[:]))
         nc.vector.tensor_copy(xcs[:], xs[:].indirect(cand_t[:]))
+        nc.vector.tensor_copy(xqs[:], xs[:].indirect(offs_t[:]))
         nc.vector.tensor_copy(wwd[:], ww[:].rearrange("p (m t b) -> p t m b", t=PACK, b=2))
         nc.vector.tensor_copy(xcsd[:], xcs[:].rearrange("p (m t) -> p t m", t=PACK))
         nc.vector.tensor_copy(xqw[:], xw[:].bitcast(U32).indirect(offs_t[:]))
-        nc.vector.tensor_copy(wsd[:], ws[:].rearrange("p (m t) -> p t m", t=PACK))
+        for t in range(PACK):
+            nc.gpsimd.tensor_copy(wsd[:, t, :], ws[:].rearrange("p (m t) -> p t m", t=PACK)[:, t, :])
         nc.vector.tensor_copy(xcw[:], xw[:].bitcast(U32).indirect(cand_t[:]))
         nc.vector.tensor_copy(xcwd[:].bitcast(I32), xcw[:].bitcast(I32).rearrange("p (m t) -> p t m", t=PACK))
 
@@ -197,32 +197,30 @@ def tile_picked_teager8_none_po_kernel(tc, x_words, x_scales, w1_words, w1_scale
         gather_left(*last[0])
         gather_right(*early[-1])
         gather_left(*last[1])
-        ob[0] = sb.tile([P, BLK, PACK], BF16, name="ob0", align_bytes=64)
-        ob[BLK] = sb.tile([P, 2 * BLK, PACK], BF16, name="ob1", align_bytes=64)
+        ob[0] = sb.tile([P, 2 * BLK, PACK], BF16, name="ob0", align_bytes=64)
+        ob[2 * BLK] = sb.tile([P, 2 * BLK, PACK], BF16, name="ob1", align_bytes=64)
         energy(0, BLK)
         gather_right(*last[0])
         bank0 = score_block(0)
-        round_block(ob[0][:], bank0)
+        round_block(ob[0][:, 0:BLK, :], bank0)
         store_block(0, bank0)
         energy(BLK, BLK)
         gather_right(*last[1])
         bank1 = score_block(BLK)
-        round_block(ob[BLK][:, 0:BLK, :], bank1)
+        round_block(ob[0][:, BLK : 2 * BLK, :], bank1)
         store_block(BLK, bank1)
         energy(2 * BLK, BLK)
         energy(HEAD, BLK)
         bank2 = score_block(2 * BLK)
         of_last = score_last()
-        quantize_out(0, BLK)
-        round_block(ob[BLK][:, BLK : 2 * BLK, :], bank2, on_vector=True)
+        quantize_out(0, 2 * BLK)
+        round_block(ob[2 * BLK][:, 0:BLK, :], bank2, on_vector=True)
         store_block(2 * BLK, bank2)
-        quantize_out(BLK, 2 * BLK)
-        ob[HEAD] = sb.tile([P, BLK, PACK], BF16, name="ob_last", align_bytes=64)
         nc.vector.tensor_copy(
-            ob[HEAD][:].rearrange("p (c i) t -> p c t i", i=2),
+            ob[2 * BLK][:, BLK : 2 * BLK, :].rearrange("p (c i) t -> p c t i", i=2),
             of_last[:].rearrange("p t (c i) -> p c t i", i=2),
         )
-        quantize_out(HEAD, BLK)
+        quantize_out(2 * BLK, 2 * BLK)
         for q in range(4):
             queue = nc.sync if q < 2 else nc.scalar
             queue.dma_start(out_2[0, 4 * q : 4 * q + 4, :].bitcast(I32), osc[32 * q : 32 * q + 4, :].bitcast(I32))

@@ -53,9 +53,9 @@ def tile_picked_teager8_none_po_kernel(tc, x_words, x_scales, w1_words, w1_scale
             nc.sync.dma_start(xs[32 * q : 32 * q + 4, :].bitcast(I32), x_scales[0, 4 * q : 4 * q + 4, :].bitcast(I32))
         nc.sync.dma_start(offs_t[:], offs)
         nc.sync.dma_start(xw[:], x_words[0].rearrange("p n t -> p (n t)").bitcast(I32))
+        nc.sync.dma_start(g[:], gs.rearrange("(p t) o -> p (t o)", t=PACK))
         for q in range(4):
             nc.sync.dma_start(ws[32 * q : 32 * q + 4, :].bitcast(I32), w1_scales[0, 4 * q : 4 * q + 4, :].bitcast(I32))
-        nc.sync.dma_start(g[:], gs.rearrange("(p t) o -> p (t o)", t=PACK))
         nc.sync.dma_start(lf_t[:], lf)
         nc.sync.dma_start(rt_t[:], rt)
 
@@ -85,25 +85,31 @@ def tile_picked_teager8_none_po_kernel(tc, x_words, x_scales, w1_words, w1_scale
             nc.scalar.activation(hg[t], g[:, t : t + 1].to_broadcast([P, S]), COPY, scale=0.5)
         nc.scalar.activation(hg_rest[:], g[:, WHOLE:PACK].unsqueeze(2).to_broadcast([P, PACK - WHOLE, HEAD]), COPY, scale=0.5)
 
-        yp = [ps.tile([P, S], F32, name="yp%d" % t) for t in range(PACK)]
+        ybanks = []
         for t in range(PACK):
-            nc.tensor.matmul_mx(
-                out=yp[t][:],
-                lhsT=wwd[:, t].rearrange("p m b -> p (m b)").bitcast(FP4X4),
-                lhsT_scale=wsd[:, t, :],
-                rhs=xqw[:].bitcast(FP8X4),
-                rhs_scale=xqs[:],
-                start=True,
-                stop=True,
-            )
-            nc.scalar.activation(win[t][:, 0:S], yp[t][:], COPY)
+            width = S // 2 if t == 0 else S
+            for c0 in range(0, S, width):
+                yp = ps.tile([P, width], F32, name="yp%d_%d" % (t, c0), tag="bank", bufs=8)
+                nc.tensor.matmul_mx(
+                    out=yp[:],
+                    lhsT=wwd[:, t].rearrange("p m b -> p (m b)").bitcast(FP4X4),
+                    lhsT_scale=wsd[:, t, :],
+                    rhs=xqw[:, c0 : c0 + width].bitcast(FP8X4),
+                    rhs_scale=xqs[:, c0 : c0 + width],
+                    start=True,
+                    stop=True,
+                )
+                nc.scalar.activation(win[t][:, c0 : c0 + width], yp[:], COPY)
+                ybanks.append((t, c0, width, yp))
 
         hsq = {}
         for c0, n in ((0, BLK), (BLK, HEAD)):
             sq = sb.tile([P, PACK, n], F32, name="sq%d" % c0, align_bytes=64)
             hsq[c0] = sb.tile([P, PACK, n], F32, name="hsq%d" % c0, align_bytes=64)
-            for t in range(PACK):
-                nc.scalar.activation(sq[:, t, :], yp[t][:, c0 : c0 + n], SQUARE)
+            for t, y0, width, yp in ybanks:
+                lo, hi = max(c0, y0), min(c0 + n, y0 + width)
+                if lo < hi:
+                    nc.scalar.activation(sq[:, t, lo - c0 : hi - c0], yp[:, lo - y0 : hi - y0], SQUARE)
             for t in range(PACK):
                 nc.scalar.activation(hsq[c0][:, t, :], sq[:, t, :], COPY, scale=hg[t][:, 0:1])
 
@@ -153,7 +159,7 @@ def tile_picked_teager8_none_po_kernel(tc, x_words, x_scales, w1_words, w1_scale
 
         def score_block(c0):
             zw, zs = quantize_energy(c0, BLK)
-            bank = ps.tile([P, PACK, BLK], F32, name="op%d" % c0, tag="op", bufs=4)
+            bank = ps.tile([P, PACK, BLK], F32, name="op%d" % c0, tag="bank", bufs=8)
             for t in range(PACK):
                 score(bank[:, t, :], t, zw[:], zs[:])
             return bank
@@ -174,7 +180,7 @@ def tile_picked_teager8_none_po_kernel(tc, x_words, x_scales, w1_words, w1_scale
             zw, zs = quantize_energy(HEAD, BLK)
             of = sb.tile([P, PACK, BLK], F32, name="of_last", align_bytes=64)
             for t0 in (0, 2):
-                bank = ps.tile([P, 2, BLK], F32, name="op_last%d" % t0, tag="op", bufs=4)
+                bank = ps.tile([P, 2, BLK], F32, name="op_last%d" % t0, tag="bank", bufs=8)
                 for t in (t0, t0 + 1):
                     score(bank[:, t - t0, :], t, zw[:], zs[:])
                 nc.scalar.activation(of[:, t0 : t0 + 2, :], bank[:], COPY, scale=OUT_SCALE)
@@ -205,13 +211,13 @@ def tile_picked_teager8_none_po_kernel(tc, x_words, x_scales, w1_words, w1_scale
         round_block(ob[0][:, 0:BLK, :], bank0)
         store_block(0, bank0)
         energy(BLK, BLK)
-        gather_right(*last[1])
+        energy(2 * BLK, BLK)
         bank1 = score_block(BLK)
         round_block(ob[0][:, BLK : 2 * BLK, :], bank1)
         store_block(BLK, bank1)
-        energy(2 * BLK, BLK)
-        energy(HEAD, BLK)
+        gather_right(*last[1])
         bank2 = score_block(2 * BLK)
+        energy(HEAD, BLK)
         of_last = score_last()
         quantize_out(0, 2 * BLK)
         round_block(ob[2 * BLK][:, 0:BLK, :], bank2, on_vector=True)

from contextlib import ExitStack

import concourse.mybir as mybir

K, T, S, H, C = 512, 2048, 512, 512, 512
FLOPS = 2 * K * H * S + 2 * K * C * S

F32 = mybir.dt.float32
BF16 = mybir.dt.bfloat16
I32 = mybir.dt.int32
U32 = mybir.dt.uint32
U16 = mybir.dt.uint16
U8 = mybir.dt.uint8
FP8X4 = mybir.dt.float8_e4m3fn_x4
FP4X4 = mybir.dt.float4_e2m1fn_x4
MULT = mybir.AluOpType.mult
SUB = mybir.AluOpType.subtract
COPY = mybir.ActivationFunctionType.Copy
SQUARE = mybir.ActivationFunctionType.Square

P = 128
PACK = 4
BLK = 128
HEAD = S - BLK
WHOLE = 2
OUT_SCALE = 0.0625


def tile_picked_teager8_none_po_kernel(tc, x_words, x_scales, w1_words, w1_scales, gs, offs, lf, rt, cand, out_0, out_1, out_2):
    nc = tc.nc
    with ExitStack() as ctx:
        lists = ctx.enter_context(tc.tile_pool(name="lists", bufs=1))
        sb = ctx.enter_context(tc.tile_pool(name="sb", bufs=1))
        ps = ctx.enter_context(tc.psum_pool(name="ps", bufs=1))

        offs_t = lists.tile([P, S // 16], U16, name="offs_t")
        cand_t = lists.tile([P, C // 16], U16, name="cand_t")
        lf_t = lists.tile([P, S // 16], U16, name="lf_t")
        rt_t = lists.tile([P, S // 16], U16, name="rt_t")

        xw = sb.tile([P, T], I32, name="xw", align_bytes=64)
        xs = sb.tile([P, T], U8, name="xs", align_bytes=64)
        ww = sb.tile([P, 2 * H], U8, name="ww", align_bytes=64)
        ws = sb.tile([P, H], U8, name="ws", align_bytes=64)
        g = sb.tile([P, PACK], F32, name="g", align_bytes=64)

        nc.vector.memset(xs[:].bitcast(I32), 0)
        nc.gpsimd.memset(ws[:].bitcast(I32), 0)

        nc.sync.dma_start(ww[:].bitcast(I32), w1_words[0].bitcast(I32))
        nc.sync.dma_start(cand_t[:], cand)
        for q in range(4):
            nc.sync.dma_start(xs[32 * q : 32 * q + 4, :].bitcast(I32), x_scales[0, 4 * q : 4 * q + 4, :].bitcast(I32))
        nc.sync.dma_start(offs_t[:], offs)
        nc.sync.dma_start(xw[:], x_words[0].rearrange("p n t -> p (n t)").bitcast(I32))
        nc.sync.dma_start(g[:], gs.rearrange("(p t) o -> p (t o)", t=PACK))
        for q in range(4):
            nc.sync.dma_start(ws[32 * q : 32 * q + 4, :].bitcast(I32), w1_scales[0, 4 * q : 4 * q + 4, :].bitcast(I32))
        nc.sync.dma_start(lf_t[:], lf)
        nc.sync.dma_start(rt_t[:], rt)

        wwd = sb.tile([P, PACK, P, 2], U8, name="wwd", align_bytes=64)
        wsd = sb.tile([P, PACK, P], U8, name="wsd", align_bytes=64)
        xqw = sb.tile([P, S], U32, name="xqw", align_bytes=64)
        xqs = sb.tile([P, S], U8, name="xqs", align_bytes=64)
        xcw = sb.tile([P, C], U32, name="xcw", align_bytes=64)
        xcs = sb.tile([P, C], U8, name="xcs", align_bytes=64)
        xcwd = sb.tile([P, PACK, P], U32, name="xcwd", align_bytes=64)
        xcsd = sb.tile([P, PACK, P], U8, name="xcsd", align_bytes=64)

        nc.vector.tensor_copy(xcs[:], xs[:].indirect(cand_t[:]))
        nc.vector.tensor_copy(xqs[:], xs[:].indirect(offs_t[:]))
        nc.vector.tensor_copy(wwd[:], ww[:].rearrange("p (m t b) -> p t m b", t=PACK, b=2))
        nc.vector.tensor_copy(xcsd[:], xcs[:].rearrange("p (m t) -> p t m", t=PACK))
        nc.vector.tensor_copy(xqw[:], xw[:].bitcast(U32).indirect(offs_t[:]))
        for t in range(PACK):
            nc.gpsimd.tensor_copy(wsd[:, t, :], ws[:].rearrange("p (m t) -> p t m", t=PACK)[:, t, :])
        nc.vector.tensor_copy(xcw[:], xw[:].bitcast(U32).indirect(cand_t[:]))
        nc.vector.tensor_copy(xcwd[:].bitcast(I32), xcw[:].bitcast(I32).rearrange("p (m t) -> p t m", t=PACK))

        win = [sb.tile([P, 2 * S if t < WHOLE else S], F32, name="win%d" % t, align_bytes=64) for t in range(PACK)]
        hg_rest = sb.tile([P, PACK - WHOLE, HEAD], F32, name="hg_rest", align_bytes=64)
        hg = [win[(t + 1) % WHOLE][:, S : 2 * S] for t in range(WHOLE)] + [hg_rest[:, t, :] for t in range(PACK - WHOLE)]
        for t in range(WHOLE):
            nc.scalar.activation(hg[t], g[:, t : t + 1].to_broadcast([P, S]), COPY, scale=0.5)
        nc.scalar.activation(hg_rest[:], g[:, WHOLE:PACK].unsqueeze(2).to_broadcast([P, PACK - WHOLE, HEAD]), COPY, scale=0.5)

        ybanks = []
        for t in range(PACK):
            width = S // 2 if t == 0 else S
            for c0 in range(0, S, width):
                yp = ps.tile([P, width], F32, name="yp%d_%d" % (t, c0), tag="bank", bufs=8)
                nc.tensor.matmul_mx(
                    out=yp[:],
                    lhsT=wwd[:, t].rearrange("p m b -> p (m b)").bitcast(FP4X4),
                    lhsT_scale=wsd[:, t, :],
                    rhs=xqw[:, c0 : c0 + width].bitcast(FP8X4),
                    rhs_scale=xqs[:, c0 : c0 + width],
                    start=True,
                    stop=True,
                )
                nc.scalar.activation(win[t][:, c0 : c0 + width], yp[:], COPY)
                ybanks.append((t, c0, width, yp))

        hsq = {}
        for c0, n in ((0, BLK), (BLK, HEAD)):
            sq = sb.tile([P, PACK, n], F32, name="sq%d" % c0, align_bytes=64)
            hsq[c0] = sb.tile([P, PACK, n], F32, name="hsq%d" % c0, align_bytes=64)
            for t, y0, width, yp in ybanks:
                lo, hi = max(c0, y0), min(c0 + n, y0 + width)
                if lo < hi:
                    nc.scalar.activation(sq[:, t, lo - c0 : hi - c0], yp[:, lo - y0 : hi - y0], SQUARE)
            for t in range(PACK):
                nc.scalar.activation(hsq[c0][:, t, :], sq[:, t, :], COPY, scale=hg[t][:, 0:1])

        ow = sb.tile([P, S], U32, name="ow", align_bytes=64)
        osc = sb.tile([P, S], U8, name="osc", align_bytes=64)
        out0 = out_0.rearrange("(p t) j -> p t j", t=PACK)
        out1 = out_1[0].rearrange("p n t -> p (n t)").bitcast(I32)

        prod = sb.tile([P, PACK, S], F32, name="prod", align_bytes=64)
        left = {}
        zb = {}
        ob = {}

        def gather_left(t, c0, n):
            left[t, c0] = sb.tile([P, n], F32, name="left%d_%d" % (t, c0), tag="left", bufs=3, align_bytes=64)
            nc.vector.tensor_tensor(left[t, c0][:], win[t][:].indirect(lf_t[:, c0 // 16 : (c0 + n) // 16]), hg[t][:, 0:n], MULT)

        def gather_right(t, c0, n):
            nc.vector.tensor_tensor(prod[:, t, c0 : c0 + n], win[t][:].indirect(rt_t[:, c0 // 16 : (c0 + n) // 16]), left[t, c0][:], MULT)

        def energy(c0, n):
            h0 = min(c0, BLK)
            zb[c0] = sb.tile([P, n, PACK], BF16, name="zb%d" % c0, align_bytes=64)
            nc.vector.tensor_tensor(
                zb[c0][:].rearrange("p (c i) t -> p c t i", i=2),
                hsq[h0][:, :, c0 - h0 : c0 - h0 + n].rearrange("p t (c i) -> p c t i", i=2),
                prod[:, :, c0 : c0 + n].rearrange("p t (c i) -> p c t i", i=2),
                SUB,
            )

        def quantize_energy(c0, n):
            zw = sb.tile([P, n], U32, name="zw%d" % c0, align_bytes=64)
            zs = sb.tile([P, n], U8, name="zs%d" % c0, align_bytes=64)
            nc.vector.quantize_mx(out=zw[:].bitcast(FP8X4), scales=zs[:], in_=zb[c0][:].rearrange("p n t -> p (n t)"))
            return zw, zs

        def score(out, t, zw, zs):
            nc.tensor.matmul_mx(
                out=out,
                lhsT=xcwd[:, t, :].bitcast(FP8X4),
                lhsT_scale=xcsd[:, t, :],
                rhs=zw.bitcast(FP8X4),
                rhs_scale=zs,
                start=True,
                stop=True,
            )

        def score_block(c0):
            zw, zs = quantize_energy(c0, BLK)
            bank = ps.tile([P, PACK, BLK], F32, name="op%d" % c0, tag="bank", bufs=8)
            for t in range(PACK):
                score(bank[:, t, :], t, zw[:], zs[:])
            return bank

        def round_block(dst, bank, on_vector=False):
            woven = bank[:].rearrange("p t n -> p n t")
            if on_vector:
                nc.vector.tensor_scalar(dst, woven, OUT_SCALE, None, MULT)
            else:
                nc.scalar.activation(dst, woven, COPY, scale=OUT_SCALE)

        def store_block(c0, bank):
            of = sb.tile([P, PACK, BLK], F32, name="of%d" % c0, align_bytes=64)
            nc.scalar.activation(of[:], bank[:], COPY, scale=OUT_SCALE)
            nc.sync.dma_start(out0[:, :, c0 : c0 + BLK], of[:])

        def score_last():
            zw, zs = quantize_energy(HEAD, BLK)
            of = sb.tile([P, PACK, BLK], F32, name="of_last", align_bytes=64)
            for t0 in (0, 2):
                bank = ps.tile([P, 2, BLK], F32, name="op_last%d" % t0, tag="bank", bufs=8)
                for t in (t0, t0 + 1):
                    score(bank[:, t - t0, :], t, zw[:], zs[:])
                nc.scalar.activation(of[:, t0 : t0 + 2, :], bank[:], COPY, scale=OUT_SCALE)
            nc.sync.dma_start(out0[:, :, HEAD:S], of[:])
            return of

        def quantize_out(c0, n):
            cols = slice(c0, c0 + n)
            nc.vector.quantize_mx(out=ow[:, cols].bitcast(FP8X4), scales=osc[:, cols], in_=ob[c0][:].rearrange("p n t -> p (n t)"))
            nc.sync.dma_start(out1[:, cols], ow[:, cols].bitcast(I32))

        whole = [(t, 0, S) for t in range(WHOLE)]
        head = [(t, 0, HEAD) for t in range(WHOLE, PACK)]
        last = [(t, HEAD, BLK) for t in range(WHOLE, PACK)]
        early = whole + head
        gather_left(*early[0])
        for i in range(1, PACK):
            gather_left(*early[i])
            gather_right(*early[i - 1])
        gather_left(*last[0])
        gather_right(*early[-1])
        gather_left(*last[1])
        ob[0] = sb.tile([P, 2 * BLK, PACK], BF16, name="ob0", align_bytes=64)
        ob[2 * BLK] = sb.tile([P, 2 * BLK, PACK], BF16, name="ob1", align_bytes=64)
        energy(0, BLK)
        gather_right(*last[0])
        bank0 = score_block(0)
        round_block(ob[0][:, 0:BLK, :], bank0)
        store_block(0, bank0)
        energy(BLK, BLK)
        energy(2 * BLK, BLK)
        bank1 = score_block(BLK)
        round_block(ob[0][:, BLK : 2 * BLK, :], bank1)
        store_block(BLK, bank1)
        gather_right(*last[1])
        bank2 = score_block(2 * BLK)
        energy(HEAD, BLK)
        of_last = score_last()
        quantize_out(0, 2 * BLK)
        round_block(ob[2 * BLK][:, 0:BLK, :], bank2, on_vector=True)
        store_block(2 * BLK, bank2)
        nc.vector.tensor_copy(
            ob[2 * BLK][:, BLK : 2 * BLK, :].rearrange("p (c i) t -> p c t i", i=2),
            of_last[:].rearrange("p t (c i) -> p c t i", i=2),
        )
        quantize_out(2 * BLK, 2 * BLK)
        for q in range(4):
            queue = nc.sync if q < 2 else nc.scalar
            queue.dma_start(out_2[0, 4 * q : 4 * q + 4, :].bitcast(I32), osc[32 * q : 32 * q + 4, :].bitcast(I32))
